import numpy as np
import ml_dtypes

BF16 = ml_dtypes.bfloat16


def bf(x):
    return np.asarray(x, np.float32).astype(BF16)


def f32(x):
    return np.asarray(x, np.float32)


def f64(x):
    return np.asarray(x).astype(np.float64)


def striped(idx):
    return np.concatenate([l.reshape(-1, 16).T for l in idx])


def rows(idx, k):
    return np.tile(np.repeat(idx, 16, axis=0), (k // (16 * 8), 1))


K, S, V, N, M = 512, 2048, 1024, 1024, 128


def setup_inputs():
    return {"base": bf(np.random.standard_normal((K, S))), "v": bf(np.random.standard_normal((K, V))), "w": bf(np.random.standard_normal((K, M)) / np.sqrt(K)), "offs": striped(np.stack([np.random.permutation(S)[:N] for _ in range(8)]))}


def reference(base, v, w, offs):
    idx = np.stack([g.T.reshape(-1) for g in np.split(offs, 8)])
    x = f64(base).copy()
    np.put_along_axis(x, rows(idx, len(x)), f64(v), axis=1)
    y = f64(w).T @ x
    return y

@@ -1,0 +1,64 @@
+import concourse.mybir as mybir
+
+BF16, F32, U16 = mybir.dt.bfloat16, mybir.dt.float32, mybir.dt.uint16
+
+ROWS, COLUMNS, ENTRIES, M = 512, 2048, 1024, 128
+P = 128
+BLOCKS = ROWS // P
+PIECE = 512
+BANK = 512
+
+FLOPS = 2 * ROWS * M * COLUMNS
+
+
+def tile_lookup_put_copy_none_kernel(tc, base, v, w, offs, out):
+    nc = tc.nc
+    with (
+        tc.tile_pool(name="held", bufs=1) as held,
+        tc.psum_pool(name="sums", bufs=1) as sums,
+    ):
+        offsets = held.tile([P, ENTRIES // 16], U16, name="offsets")
+        nc.sync.dma_start(offsets[:], offs)
+
+        weights = held.tile([P, BLOCKS * M], BF16, name="weights")
+
+        x, values = [], []
+        for b in range(BLOCKS):
+            x_block = held.tile([P, COLUMNS], BF16, name=f"x{b}")
+            v_block = held.tile([P, ENTRIES], BF16, name=f"v{b}")
+            nc.sync.dma_start(x_block[:], base[b * P : (b + 1) * P, :])
+            nc.scalar.dma_start(v_block[:], v[b * P : (b + 1) * P, :])
+            if b == 0:
+                nc.scalar.dma_start(
+                    weights[:].rearrange("p (b m) -> p b m", b=BLOCKS),
+                    w.rearrange("(b p) m -> p b m", p=P),
+                )
+            x.append(x_block)
+            values.append(v_block)
+
+        banks = [
+            sums.tile([P, BANK], F32, name=f"bank{c}") for c in range(COLUMNS // BANK)
+        ]
+
+        for b in range(BLOCKS):
+            for first in range(0, ENTRIES, PIECE):
+                nc.vector.tensor_copy(
+                    x[b][:].indirect(offsets[:, first // 16 : (first + PIECE) // 16]),
+                    values[b][:, first : first + PIECE],
+                )
+            for c, bank in enumerate(banks):
+                nc.tensor.matmul(
+                    bank[:],
+                    weights[:, b * M : (b + 1) * M],
+                    x[b][:, c * BANK : (c + 1) * BANK],
+                    start=(b == 0),
+                    stop=(b == BLOCKS - 1),
+                )
+
+        for c, bank in enumerate(banks):
+            staged = held.tile([P, BANK], F32, name=f"staged{c}")
+            if c % 2 == 0:
+                nc.scalar.copy(staged[:], bank[:])
+            else:
+                nc.vector.tensor_copy(staged[:], bank[:])
+            nc.sync.dma_start(out[:, c * BANK : (c + 1) * BANK], staged[:])

@@ -7,6 +7,7 @@ P = 128
 BLOCKS = ROWS // P
 PIECE = 512
 BANK = 512
+WARM_UPS = 14
 
 FLOPS = 2 * ROWS * M * COLUMNS
 
@@ -40,6 +41,8 @@ def tile_lookup_put_copy_none_kernel(tc, base, v, w, offs, out):
             sums.tile([P, BANK], F32, name=f"bank{c}") for c in range(COLUMNS // BANK)
         ]
 
+        warm_bank = sums.tile([P, BANK], F32, name="warm_bank")
+
         for b in range(BLOCKS):
             for first in range(0, ENTRIES, PIECE):
                 nc.vector.tensor_copy(
@@ -54,6 +57,9 @@ def tile_lookup_put_copy_none_kernel(tc, base, v, w, offs, out):
                     start=(b == 0),
                     stop=(b == BLOCKS - 1),
                 )
+            if b == BLOCKS - 2:
+                for c in range(WARM_UPS):
+                    nc.tensor.matmul(warm_bank[:], weights[:, b * M : (b + 1) * M], x[b][:, :BANK])
 
         for c, bank in enumerate(banks):
             staged = held.tile([P, BANK], F32, name=f"staged{c}")

@@ -19,7 +19,6 @@ def tile_lookup_put_copy_none_kernel(tc, base, v, w, offs, out):
         tc.psum_pool(name="sums", bufs=1) as sums,
     ):
         offsets = held.tile([P, ENTRIES // 16], U16, name="offsets")
-        nc.sync.dma_start(offsets[:], offs)
 
         weights = held.tile([P, BLOCKS * M], BF16, name="weights")
 
@@ -28,9 +27,11 @@ def tile_lookup_put_copy_none_kernel(tc, base, v, w, offs, out):
             x_block = held.tile([P, COLUMNS], BF16, name=f"x{b}")
             v_block = held.tile([P, ENTRIES], BF16, name=f"v{b}")
             nc.sync.dma_start(x_block[:], base[b * P : (b + 1) * P, :])
-            nc.scalar.dma_start(v_block[:], v[b * P : (b + 1) * P, :])
             if b == 0:
-                nc.scalar.dma_start(
+                nc.sync.dma_start(offsets[:], offs)
+            nc.sync.dma_start(v_block[:], v[b * P : (b + 1) * P, :])
+            if b == 0:
+                nc.sync.dma_start(
                     weights[:].rearrange("p (b m) -> p b m", b=BLOCKS),
                     w.rearrange("(b p) m -> p b m", p=P),
                 )

@@ -64,8 +64,10 @@ def tile_lookup_put_copy_none_kernel(tc, base, v, w, offs, out):
 
         for c, bank in enumerate(banks):
             staged = held.tile([P, BANK], F32, name=f"staged{c}")
+            columns = out[:, c * BANK : (c + 1) * BANK]
             if c % 2 == 0:
                 nc.scalar.copy(staged[:], bank[:])
+                nc.scalar.dma_start(columns, staged[:])
             else:
                 nc.vector.tensor_copy(staged[:], bank[:])
-            nc.sync.dma_start(out[:, c * BANK : (c + 1) * BANK], staged[:])
+                nc.sync.dma_start(columns, staged[:])

import concourse.mybir as mybir

BF16, F32, U16 = mybir.dt.bfloat16, mybir.dt.float32, mybir.dt.uint16

ROWS, COLUMNS, ENTRIES, M = 512, 2048, 1024, 128
P = 128
BLOCKS = ROWS // P
PIECE = 512
BANK = 512
WARM_UPS = 14

FLOPS = 2 * ROWS * M * COLUMNS


def tile_lookup_put_copy_none_kernel(tc, base, v, w, offs, out):
    nc = tc.nc
    with (
        tc.tile_pool(name="held", bufs=1) as held,
        tc.psum_pool(name="sums", bufs=1) as sums,
    ):
        offsets = held.tile([P, ENTRIES // 16], U16, name="offsets")

        weights = held.tile([P, BLOCKS * M], BF16, name="weights")

        x, values = [], []
        for b in range(BLOCKS):
            x_block = held.tile([P, COLUMNS], BF16, name=f"x{b}")
            v_block = held.tile([P, ENTRIES], BF16, name=f"v{b}")
            nc.sync.dma_start(x_block[:], base[b * P : (b + 1) * P, :])
            if b == 0:
                nc.sync.dma_start(offsets[:], offs)
            nc.sync.dma_start(v_block[:], v[b * P : (b + 1) * P, :])
            if b == 0:
                nc.sync.dma_start(
                    weights[:].rearrange("p (b m) -> p b m", b=BLOCKS),
                    w.rearrange("(b p) m -> p b m", p=P),
                )
            x.append(x_block)
            values.append(v_block)

        banks = [
            sums.tile([P, BANK], F32, name=f"bank{c}") for c in range(COLUMNS // BANK)
        ]

        warm_bank = sums.tile([P, BANK], F32, name="warm_bank")

        for b in range(BLOCKS):
            for first in range(0, ENTRIES, PIECE):
                nc.vector.tensor_copy(
                    x[b][:].indirect(offsets[:, first // 16 : (first + PIECE) // 16]),
                    values[b][:, first : first + PIECE],
                )
            for c, bank in enumerate(banks):
                nc.tensor.matmul(
                    bank[:],
                    weights[:, b * M : (b + 1) * M],
                    x[b][:, c * BANK : (c + 1) * BANK],
                    start=(b == 0),
                    stop=(b == BLOCKS - 1),
                )
            if b == BLOCKS - 2:
                for c in range(WARM_UPS):
                    nc.tensor.matmul(warm_bank[:], weights[:, b * M : (b + 1) * M], x[b][:, :BANK])

        for c, bank in enumerate(banks):
            staged = held.tile([P, BANK], F32, name=f"staged{c}")
            columns = out[:, c * BANK : (c + 1) * BANK]
            if c % 2 == 0:
                nc.scalar.copy(staged[:], bank[:])
                nc.scalar.dma_start(columns, staged[:])
            else:
                nc.vector.tensor_copy(staged[:], bank[:])
                nc.sync.dma_start(columns, staged[:])
